import numpy as np, ml_dtypes
CORES = [4,12,20,28,36,44,0,8,16,24,32,40]
N = 12
G1 = [0,1,2,3,4,5]
G2 = [0,1,2,3,4,5,6,7,8,9,10,11]
def setup_inputs(rng):
    return {"x1": rng.standard_normal((N, 128, 510), dtype=np.float32), "x2": rng.standard_normal((N, 128, 64), dtype=np.float32).astype(ml_dtypes.bfloat16)}
def reference(x1, x2):
    out = {}
    y = np.full((N, 128, 85), np.nan, x1.dtype)
    s = x1[G1].sum(axis=0, dtype=np.float64).astype(x1.dtype)
    for i, r in enumerate(G1):
        y[r] = s[:, 85 * i:85 * i + 85]
    out["y1"] = y
    y = np.full((N, 128, 64), np.nan, x2.dtype)
    for i, r in enumerate(G2):
        y[G2[(i + 1) % 12]] = x2[r]
    out["y2"] = y
    return out

@@ -1,0 +1,184 @@
+from concourse.bass import DstId, RemoteDMATransfer
+
+NSIM = 48
+NB = 6
+W = 85
+
+SCRATCH = {
+    "blk": ("dram", [NB, 128, W], "float32"),
+    "pin": ("dram", [3, 128, W], "float32"),
+    "fin": ("dram", [4, 128, W], "float32"),
+    "res": ("dram", [128, W], "float32"),
+    "x2s": ("dram", [128, 64], "bfloat16"),
+    "x2h": ("dram", [128, 64], "bfloat16"),
+    "x2l": ("dram", [128, 64], "bfloat16"),
+}
+SEMAPHORES = ["ld_x2", "ld_b", "ld_a", "sent", "p_arr", "f_arr", "r_arr", "h_arr", "x2_arr", "st1", "st2"]
+
+
+def _bits(mask):
+    return [e for e in range(mask.bit_length()) if (mask >> e) & 1]
+
+
+def _mask_of(engines):
+    m = 0
+    for e in engines:
+        m |= 1 << e
+    return m
+
+
+def _pow2(n):
+    k = 1
+    while 2 * k <= n:
+        k *= 2
+    return k
+
+
+def _share(topo, src, dsts):
+    allowed = [_bits(topo.mask(src, d)) for d in dsts]
+    least = min(len(a) for a in allowed)
+    narrow = [k for k in range(len(dsts)) if len(allowed[k]) == least]
+    wide = [k for k in range(len(dsts)) if len(allowed[k]) != least]
+    masks = [0] * len(dsts)
+    used = []
+    for group in (narrow, wide):
+        if not group:
+            continue
+        pool = [e for e in allowed[group[0]] if e not in used]
+        n = _pow2(len(pool) // len(group))
+        for pos, k in enumerate(group):
+            mine = pool[pos * n:(pos + 1) * n]
+            masks[k] = _mask_of(mine)
+            used += mine
+    return masks
+
+
+def _layout(T, topo):
+    chips = sorted({topo.chip(c) for c in T.cores})
+    on_chip = {ch: [c for c in range(NSIM) if topo.chip(c) == ch] for ch in chips}
+    mate = {ch: [b for b in chips if topo.mates(ch, b)][0] for ch in chips}
+    m1 = [T.cores[r] for r in T.tables["G1"]]
+    P, F, H = {}, {}, {}
+    for ch in chips:
+        free = [c for c in on_chip[ch] if c not in T.cores]
+        port = [c for c in free if topo.may_write(c, on_chip[mate[ch]][0])]
+        r1 = [c for c in m1 if topo.chip(c) == ch][0]
+        P[ch] = [c for c in port if topo.die(c) == topo.die(r1)][0]
+        free.remove(P[ch])
+        port.remove(P[ch])
+        for s in [c for c in T.cores if topo.chip(c) == ch]:
+            H[s] = ([c for c in port if topo.die(c) == topo.die(s)] + port)[0]
+            free.remove(H[s])
+            port.remove(H[s])
+        F[ch] = ([c for c in free if c not in port and topo.die(c) == topo.die(r1)] + free)[0]
+    near = {}
+    for j in range(NB):
+        cj = topo.chip(m1[j])
+        near[j] = [i for i in range(NB) if topo.chip(m1[i]) == cj or topo.same_plane(topo.chip(m1[i]), cj)]
+    return {"mate": mate, "m1": m1, "P": P, "F": F, "H": H, "near": near}
+
+
+def _call(topo, L, i, far):
+    m1, near = L["m1"], L["near"]
+    out = []
+    for j in range(NB):
+        cj = topo.chip(m1[j])
+        if far and i not in near[j]:
+            others = [k for k in range(NB) if k not in near[j]]
+            out.append((j, L["P"][L["mate"][cj]], "pin", others.index(i), "p_arr"))
+        if not far and i in near[j]:
+            out.append((j, L["F"][cj], "fin", near[j].index(i), "f_arr"))
+    out.sort(key=lambda t: topo.chip(t[1]) == topo.chip(m1[i]))
+    masks = _share(topo, m1[i], [t[1] for t in out])
+    return [t + (mk,) for t, mk in zip(out, masks)]
+
+
+def _expected(topo, L, core, far):
+    return sum(len(_bits(t[5])) for i in range(NB) for t in _call(topo, L, i, far) if t[1] == core)
+
+
+def _dst(topo, c):
+    rid, pid, _ = topo.addr(c)
+    return DstId(rid=rid, pnc=pid)
+
+
+def _copy(g, T, topo, src, dst, out_ap, in_ap, remote_sem):
+    rid, pid, _ = topo.addr(dst)
+    mask = topo.mask(src, dst)
+    g.remote_dma(out_ap, in_ap, remote_sem, T.sem.sent, pid, rid, mask)
+    return len(_bits(mask))
+
+
+def _fold(g, T, topo, src, dst, out_ap, in_aps, remote_sem):
+    mask = topo.mask(src, dst)
+    g.remote_dma_fused([RemoteDMATransfer(dst_ids=[_dst(topo, dst)], dma_engine_mask=mask, remote_sem=remote_sem,
+                                          srcs=in_aps, dsts=[out_ap], alu_op=1)], local_sem=T.sem.sent)
+    return len(_bits(mask))
+
+
+def rank_program(g, core, T, topo):
+    L = _layout(T, topo)
+    sem = T.sem
+    m1 = L["m1"]
+    g2 = [T.cores[r] for r in T.tables["G2"]]
+    nxt = {g2[k]: g2[(k + 1) % len(g2)] for k in range(len(g2))}
+    prv = {d: s for s, d in nxt.items()}
+    ch = topo.chip(core)
+    sent = 0
+
+    if T.rank_of(core) is not None:
+        queues = [g.sync, g.scalar]
+        calls = []
+        if core in nxt:
+            g.sync.dma_start(T.x2s[:], T.x2[:]).then_inc(sem.ld_x2, 16)
+        if core in m1:
+            i = m1.index(core)
+            n = 1
+            for far, ld in ((True, sem.ld_b), (False, sem.ld_a)):
+                call = _call(topo, L, i, far)
+                calls.append((call, ld))
+                for t in call:
+                    j = t[0]
+                    queues[n % 2].dma_start(T.blk[j], T.x1[:, W * j:W * (j + 1)]).then_inc(ld, 16)
+                    n += 1
+        if core in nxt:
+            g.wait_ge(sem.ld_x2, 16)
+            if topo.may_write(core, nxt[core]):
+                sent += _copy(g, T, topo, core, nxt[core], T.x2l[:], T.x2s[:], sem.x2_arr)
+            else:
+                sent += _copy(g, T, topo, core, L["H"][core], T.x2h[:], T.x2s[:], sem.h_arr)
+        for call, ld in calls:
+            g.wait_ge(ld, 16 * len(call))
+            g.remote_dma_fused([RemoteDMATransfer(dst_ids=[_dst(topo, d)], dma_engine_mask=mk, remote_sem=sem[sm],
+                                                  src=T.blk[j], dst=T[buf][slot])
+                                for j, d, buf, slot, sm, mk in call], local_sem=sem.sent)
+            sent += sum(len(_bits(t[5])) for t in call)
+        if core in m1:
+            g.sync.wait_ge(sem.r_arr, len(_bits(topo.mask(L["F"][ch], core))))
+            g.sync.dma_start(T.y1[:], T.res[:]).then_inc(sem.st1, 16)
+            g.sync.wait_ge(sem.st1, 16)
+        if core in prv:
+            s = prv[core]
+            last = s if topo.may_write(s, core) else L["H"][s]
+            g.scalar.wait_ge(sem.x2_arr, len(_bits(topo.mask(last, core))))
+            g.scalar.dma_start(T.y2[:], T.x2l[:]).then_inc(sem.st2, 16)
+            g.scalar.wait_ge(sem.st2, 16)
+
+    for s, h in L["H"].items():
+        if h == core and s in nxt and not topo.may_write(s, nxt[s]):
+            g.wait_ge(sem.h_arr, len(_bits(topo.mask(s, h))))
+            sent += _copy(g, T, topo, core, nxt[s], T.x2l[:], T.x2h[:], sem.x2_arr)
+
+    if core == L["P"][ch]:
+        g.wait_ge(sem.p_arr, _expected(topo, L, core, True))
+        j = [k for k in range(NB) if topo.chip(m1[k]) == L["mate"][ch]][0]
+        sent += _fold(g, T, topo, core, L["F"][L["mate"][ch]], T.fin[len(L["near"][j])],
+                      [T.pin[k] for k in range(NB - len(L["near"][j]))], sem.f_arr)
+
+    if core == L["F"][ch]:
+        j = [k for k in range(NB) if topo.chip(m1[k]) == ch][0]
+        g.wait_ge(sem.f_arr, _expected(topo, L, core, False) + len(_bits(topo.mask(L["P"][L["mate"][ch]], core))))
+        sent += _fold(g, T, topo, core, m1[j], T.res[:], [T.fin[k] for k in range(len(L["near"][j]) + 1)], sem.r_arr)
+
+    if sent:
+        g.wait_ge(sem.sent, sent)

@@ -3,6 +3,8 @@ from concourse.bass import DstId, RemoteDMATransfer
 NSIM = 48
 NB = 6
 W = 85
+GROUPS = [[0, 1, 2], [3, 4, 5]]
+X2_AT = 1
 
 SCRATCH = {
     "blk": ("dram", [NB, 128, W], "float32"),
@@ -13,7 +15,8 @@ SCRATCH = {
     "x2h": ("dram", [128, 64], "bfloat16"),
     "x2l": ("dram", [128, 64], "bfloat16"),
 }
-SEMAPHORES = ["ld_x2", "ld_b", "ld_a", "sent", "p_arr", "f_arr", "r_arr", "h_arr", "x2_arr", "st1", "st2"]
+SEMAPHORES = ["ld_x2", "sent", "p_arr", "f_arr", "r_arr", "h_arr", "x2_arr", "st1", "st2"] + [
+    "ld%d" % k for k in range(NB)]
 
 
 def _bits(mask):
@@ -67,7 +70,7 @@ def _layout(T, topo):
         free.remove(P[ch])
         port.remove(P[ch])
         for s in [c for c in T.cores if topo.chip(c) == ch]:
-            H[s] = ([c for c in port if topo.die(c) == topo.die(s)] + port)[0]
+            H[s] = ([c for c in port if topo.die(c) != topo.die(r1)] + port)[0]
             free.remove(H[s])
             port.remove(H[s])
         F[ch] = ([c for c in free if c not in port and topo.die(c) == topo.die(r1)] + free)[0]
@@ -78,23 +81,27 @@ def _layout(T, topo):
     return {"mate": mate, "m1": m1, "P": P, "F": F, "H": H, "near": near}
 
 
-def _call(topo, L, i, far):
+def _calls(topo, L, i):
     m1, near = L["m1"], L["near"]
-    out = []
+    far, close = [], []
     for j in range(NB):
         cj = topo.chip(m1[j])
-        if far and i not in near[j]:
+        if i in near[j]:
+            close.append((j, L["F"][cj], "fin", near[j].index(i), "f_arr"))
+        else:
             others = [k for k in range(NB) if k not in near[j]]
-            out.append((j, L["P"][L["mate"][cj]], "pin", others.index(i), "p_arr"))
-        if not far and i in near[j]:
-            out.append((j, L["F"][cj], "fin", near[j].index(i), "f_arr"))
-    out.sort(key=lambda t: topo.chip(t[1]) == topo.chip(m1[i]))
-    masks = _share(topo, m1[i], [t[1] for t in out])
-    return [t + (mk,) for t, mk in zip(out, masks)]
+            far.append((j, L["P"][L["mate"][cj]], "pin", others.index(i), "p_arr"))
+    here = lambda t: topo.chip(t[1]) == topo.chip(m1[i])
+    order = sorted(far, key=here) + sorted(close, key=here)
+    out = []
+    for grp in GROUPS:
+        ts = [order[k] for k in grp]
+        out.append([t + (mk,) for t, mk in zip(ts, _share(topo, m1[i], [t[1] for t in ts]))])
+    return out
 
 
-def _expected(topo, L, core, far):
-    return sum(len(_bits(t[5])) for i in range(NB) for t in _call(topo, L, i, far) if t[1] == core)
+def _expected(topo, L, core):
+    return sum(len(_bits(t[5])) for i in range(NB) for call in _calls(topo, L, i) for t in call if t[1] == core)
 
 
 def _dst(topo, c):
@@ -128,31 +135,32 @@ def rank_program(g, core, T, topo):
 
     if T.rank_of(core) is not None:
         queues = [g.sync, g.scalar]
-        calls = []
-        if core in nxt:
-            g.sync.dma_start(T.x2s[:], T.x2[:]).then_inc(sem.ld_x2, 16)
-        if core in m1:
-            i = m1.index(core)
-            n = 1
-            for far, ld in ((True, sem.ld_b), (False, sem.ld_a)):
-                call = _call(topo, L, i, far)
-                calls.append((call, ld))
-                for t in call:
+        calls = _calls(topo, L, m1.index(core)) if core in m1 else []
+        x2_at = min(X2_AT, len(calls))
+        n = 0
+        for k in range(len(calls) + 1):
+            if core in nxt and k == x2_at:
+                queues[n % 2].dma_start(T.x2s[:], T.x2[:]).then_inc(sem.ld_x2, 16)
+                n += 1
+            if k < len(calls):
+                for t in calls[k]:
                     j = t[0]
-                    queues[n % 2].dma_start(T.blk[j], T.x1[:, W * j:W * (j + 1)]).then_inc(ld, 16)
+                    queues[n % 2].dma_start(T.blk[j], T.x1[:, W * j:W * (j + 1)]).then_inc(sem["ld%d" % k], 16)
                     n += 1
-        if core in nxt:
-            g.wait_ge(sem.ld_x2, 16)
-            if topo.may_write(core, nxt[core]):
-                sent += _copy(g, T, topo, core, nxt[core], T.x2l[:], T.x2s[:], sem.x2_arr)
-            else:
-                sent += _copy(g, T, topo, core, L["H"][core], T.x2h[:], T.x2s[:], sem.h_arr)
-        for call, ld in calls:
-            g.wait_ge(ld, 16 * len(call))
-            g.remote_dma_fused([RemoteDMATransfer(dst_ids=[_dst(topo, d)], dma_engine_mask=mk, remote_sem=sem[sm],
-                                                  src=T.blk[j], dst=T[buf][slot])
-                                for j, d, buf, slot, sm, mk in call], local_sem=sem.sent)
-            sent += sum(len(_bits(t[5])) for t in call)
+        for k in range(len(calls) + 1):
+            if core in nxt and k == x2_at:
+                g.wait_ge(sem.ld_x2, 16)
+                if topo.may_write(core, nxt[core]):
+                    sent += _copy(g, T, topo, core, nxt[core], T.x2l[:], T.x2s[:], sem.x2_arr)
+                else:
+                    sent += _copy(g, T, topo, core, L["H"][core], T.x2h[:], T.x2s[:], sem.h_arr)
+            if k < len(calls):
+                call = calls[k]
+                g.wait_ge(sem["ld%d" % k], 16 * len(call))
+                g.remote_dma_fused([RemoteDMATransfer(dst_ids=[_dst(topo, d)], dma_engine_mask=mk,
+                                                      remote_sem=sem[sm], src=T.blk[j], dst=T[buf][slot])
+                                    for j, d, buf, slot, sm, mk in call], local_sem=sem.sent)
+                sent += sum(len(_bits(t[5])) for t in call)
         if core in m1:
             g.sync.wait_ge(sem.r_arr, len(_bits(topo.mask(L["F"][ch], core))))
             g.sync.dma_start(T.y1[:], T.res[:]).then_inc(sem.st1, 16)
@@ -170,14 +178,14 @@ def rank_program(g, core, T, topo):
             sent += _copy(g, T, topo, core, nxt[s], T.x2l[:], T.x2h[:], sem.x2_arr)
 
     if core == L["P"][ch]:
-        g.wait_ge(sem.p_arr, _expected(topo, L, core, True))
+        g.wait_ge(sem.p_arr, _expected(topo, L, core))
         j = [k for k in range(NB) if topo.chip(m1[k]) == L["mate"][ch]][0]
         sent += _fold(g, T, topo, core, L["F"][L["mate"][ch]], T.fin[len(L["near"][j])],
                       [T.pin[k] for k in range(NB - len(L["near"][j]))], sem.f_arr)
 
     if core == L["F"][ch]:
         j = [k for k in range(NB) if topo.chip(m1[k]) == ch][0]
-        g.wait_ge(sem.f_arr, _expected(topo, L, core, False) + len(_bits(topo.mask(L["P"][L["mate"][ch]], core))))
+        g.wait_ge(sem.f_arr, _expected(topo, L, core) + len(_bits(topo.mask(L["P"][L["mate"][ch]], core))))
         sent += _fold(g, T, topo, core, m1[j], T.res[:], [T.fin[k] for k in range(len(L["near"][j]) + 1)], sem.r_arr)
 
     if sent:

from concourse.bass import DstId, RemoteDMATransfer

NSIM = 48
NB = 6
W = 85
GROUPS = [[0, 1, 2], [3, 4, 5]]
X2_AT = 1

SCRATCH = {
    "blk": ("dram", [NB, 128, W], "float32"),
    "pin": ("dram", [3, 128, W], "float32"),
    "fin": ("dram", [4, 128, W], "float32"),
    "res": ("dram", [128, W], "float32"),
    "x2s": ("dram", [128, 64], "bfloat16"),
    "x2h": ("dram", [128, 64], "bfloat16"),
    "x2l": ("dram", [128, 64], "bfloat16"),
}
SEMAPHORES = ["ld_x2", "sent", "p_arr", "f_arr", "r_arr", "h_arr", "x2_arr", "st1", "st2"] + [
    "ld%d" % k for k in range(NB)]


def _bits(mask):
    return [e for e in range(mask.bit_length()) if (mask >> e) & 1]


def _mask_of(engines):
    m = 0
    for e in engines:
        m |= 1 << e
    return m


def _pow2(n):
    k = 1
    while 2 * k <= n:
        k *= 2
    return k


def _share(topo, src, dsts):
    allowed = [_bits(topo.mask(src, d)) for d in dsts]
    least = min(len(a) for a in allowed)
    narrow = [k for k in range(len(dsts)) if len(allowed[k]) == least]
    wide = [k for k in range(len(dsts)) if len(allowed[k]) != least]
    masks = [0] * len(dsts)
    used = []
    for group in (narrow, wide):
        if not group:
            continue
        pool = [e for e in allowed[group[0]] if e not in used]
        n = _pow2(len(pool) // len(group))
        for pos, k in enumerate(group):
            mine = pool[pos * n:(pos + 1) * n]
            masks[k] = _mask_of(mine)
            used += mine
    return masks


def _layout(T, topo):
    chips = sorted({topo.chip(c) for c in T.cores})
    on_chip = {ch: [c for c in range(NSIM) if topo.chip(c) == ch] for ch in chips}
    mate = {ch: [b for b in chips if topo.mates(ch, b)][0] for ch in chips}
    m1 = [T.cores[r] for r in T.tables["G1"]]
    P, F, H = {}, {}, {}
    for ch in chips:
        free = [c for c in on_chip[ch] if c not in T.cores]
        port = [c for c in free if topo.may_write(c, on_chip[mate[ch]][0])]
        r1 = [c for c in m1 if topo.chip(c) == ch][0]
        P[ch] = [c for c in port if topo.die(c) == topo.die(r1)][0]
        free.remove(P[ch])
        port.remove(P[ch])
        for s in [c for c in T.cores if topo.chip(c) == ch]:
            H[s] = ([c for c in port if topo.die(c) != topo.die(r1)] + port)[0]
            free.remove(H[s])
            port.remove(H[s])
        F[ch] = ([c for c in free if c not in port and topo.die(c) == topo.die(r1)] + free)[0]
    near = {}
    for j in range(NB):
        cj = topo.chip(m1[j])
        near[j] = [i for i in range(NB) if topo.chip(m1[i]) == cj or topo.same_plane(topo.chip(m1[i]), cj)]
    return {"mate": mate, "m1": m1, "P": P, "F": F, "H": H, "near": near}


def _calls(topo, L, i):
    m1, near = L["m1"], L["near"]
    far, close = [], []
    for j in range(NB):
        cj = topo.chip(m1[j])
        if i in near[j]:
            close.append((j, L["F"][cj], "fin", near[j].index(i), "f_arr"))
        else:
            others = [k for k in range(NB) if k not in near[j]]
            far.append((j, L["P"][L["mate"][cj]], "pin", others.index(i), "p_arr"))
    here = lambda t: topo.chip(t[1]) == topo.chip(m1[i])
    order = sorted(far, key=here) + sorted(close, key=here)
    out = []
    for grp in GROUPS:
        ts = [order[k] for k in grp]
        out.append([t + (mk,) for t, mk in zip(ts, _share(topo, m1[i], [t[1] for t in ts]))])
    return out


def _expected(topo, L, core):
    return sum(len(_bits(t[5])) for i in range(NB) for call in _calls(topo, L, i) for t in call if t[1] == core)


def _dst(topo, c):
    rid, pid, _ = topo.addr(c)
    return DstId(rid=rid, pnc=pid)


def _copy(g, T, topo, src, dst, out_ap, in_ap, remote_sem):
    rid, pid, _ = topo.addr(dst)
    mask = topo.mask(src, dst)
    g.remote_dma(out_ap, in_ap, remote_sem, T.sem.sent, pid, rid, mask)
    return len(_bits(mask))


def _fold(g, T, topo, src, dst, out_ap, in_aps, remote_sem):
    mask = topo.mask(src, dst)
    g.remote_dma_fused([RemoteDMATransfer(dst_ids=[_dst(topo, dst)], dma_engine_mask=mask, remote_sem=remote_sem,
                                          srcs=in_aps, dsts=[out_ap], alu_op=1)], local_sem=T.sem.sent)
    return len(_bits(mask))


def rank_program(g, core, T, topo):
    L = _layout(T, topo)
    sem = T.sem
    m1 = L["m1"]
    g2 = [T.cores[r] for r in T.tables["G2"]]
    nxt = {g2[k]: g2[(k + 1) % len(g2)] for k in range(len(g2))}
    prv = {d: s for s, d in nxt.items()}
    ch = topo.chip(core)
    sent = 0

    if T.rank_of(core) is not None:
        queues = [g.sync, g.scalar]
        calls = _calls(topo, L, m1.index(core)) if core in m1 else []
        x2_at = min(X2_AT, len(calls))
        n = 0
        for k in range(len(calls) + 1):
            if core in nxt and k == x2_at:
                queues[n % 2].dma_start(T.x2s[:], T.x2[:]).then_inc(sem.ld_x2, 16)
                n += 1
            if k < len(calls):
                for t in calls[k]:
                    j = t[0]
                    queues[n % 2].dma_start(T.blk[j], T.x1[:, W * j:W * (j + 1)]).then_inc(sem["ld%d" % k], 16)
                    n += 1
        for k in range(len(calls) + 1):
            if core in nxt and k == x2_at:
                g.wait_ge(sem.ld_x2, 16)
                if topo.may_write(core, nxt[core]):
                    sent += _copy(g, T, topo, core, nxt[core], T.x2l[:], T.x2s[:], sem.x2_arr)
                else:
                    sent += _copy(g, T, topo, core, L["H"][core], T.x2h[:], T.x2s[:], sem.h_arr)
            if k < len(calls):
                call = calls[k]
                g.wait_ge(sem["ld%d" % k], 16 * len(call))
                g.remote_dma_fused([RemoteDMATransfer(dst_ids=[_dst(topo, d)], dma_engine_mask=mk,
                                                      remote_sem=sem[sm], src=T.blk[j], dst=T[buf][slot])
                                    for j, d, buf, slot, sm, mk in call], local_sem=sem.sent)
                sent += sum(len(_bits(t[5])) for t in call)
        if core in m1:
            g.sync.wait_ge(sem.r_arr, len(_bits(topo.mask(L["F"][ch], core))))
            g.sync.dma_start(T.y1[:], T.res[:]).then_inc(sem.st1, 16)
            g.sync.wait_ge(sem.st1, 16)
        if core in prv:
            s = prv[core]
            last = s if topo.may_write(s, core) else L["H"][s]
            g.scalar.wait_ge(sem.x2_arr, len(_bits(topo.mask(last, core))))
            g.scalar.dma_start(T.y2[:], T.x2l[:]).then_inc(sem.st2, 16)
            g.scalar.wait_ge(sem.st2, 16)

    for s, h in L["H"].items():
        if h == core and s in nxt and not topo.may_write(s, nxt[s]):
            g.wait_ge(sem.h_arr, len(_bits(topo.mask(s, h))))
            sent += _copy(g, T, topo, core, nxt[s], T.x2l[:], T.x2h[:], sem.x2_arr)

    if core == L["P"][ch]:
        g.wait_ge(sem.p_arr, _expected(topo, L, core))
        j = [k for k in range(NB) if topo.chip(m1[k]) == L["mate"][ch]][0]
        sent += _fold(g, T, topo, core, L["F"][L["mate"][ch]], T.fin[len(L["near"][j])],
                      [T.pin[k] for k in range(NB - len(L["near"][j]))], sem.f_arr)

    if core == L["F"][ch]:
        j = [k for k in range(NB) if topo.chip(m1[k]) == ch][0]
        g.wait_ge(sem.f_arr, _expected(topo, L, core) + len(_bits(topo.mask(L["P"][L["mate"][ch]], core))))
        sent += _fold(g, T, topo, core, m1[j], T.res[:], [T.fin[k] for k in range(len(L["near"][j]) + 1)], sem.r_arr)

    if sent:
        g.wait_ge(sem.sent, sent)
